import numpy as np
import ml_dtypes


def mxq(x, axis, fmt="e4m3"):
    dtype, down = {"e4m3": (ml_dtypes.float8_e4m3fn, 7), "e5m2": (ml_dtypes.float8_e5m2, 14)}[fmt]
    v = np.moveaxis(np.asarray(x, np.float32).astype(ml_dtypes.bfloat16).astype(np.float64), axis, -1)
    blocks = v.reshape(v.shape[:-1] + (-1, 32))
    amax = np.abs(blocks).max(-1, keepdims=True)
    byte = np.maximum(np.where(amax > 0, np.frexp(amax)[1] - 1 + 127, 0) - down, 1)
    scale = np.exp2(byte - 127.0)
    codes = (blocks / scale).astype(np.float32).astype(dtype).astype(np.float64)
    return np.moveaxis((codes * scale).reshape(v.shape), -1, axis)


WIDE = False


def mx_kscale(k):
    if not WIDE:
        return np.ones(k)
    levels = np.array([10, -10, 5, -5, 0])
    if k % 512:
        return np.exp2(np.random.permutation(np.resize(levels, k // 32))).repeat(32)
    a = np.empty((k // 512, 16))
    for p in range(k // 512):
        a[p, :8] = np.random.permutation(np.resize(levels, 8))
        for g in range(8):
            far = levels[np.abs(levels - a[p, g]) >= 10]
            a[p, g + 8] = far[np.random.randint(len(far))]
    return np.exp2(a.ravel()).repeat(32)


def f64(x):
    return np.asarray(x).astype(np.float64)


def striped(idx):
    return np.tile(idx.reshape(-1, 16).T, (8, 1)).astype(np.uint16)


def unstriped(offs):
    return offs[:16].T.reshape(-1).astype(np.int64)


def striped8(idx):
    return np.concatenate([x.reshape(-1, 16).T for x in idx]).astype(np.uint16)


def runs(offs, k):
    lists = np.stack([offs[16 * r : 16 * r + 16].T.reshape(-1) for r in range(8)]).astype(np.int64)
    return lists[np.arange(k) % 512 // 64]


def pack_weight(w):
    k, n = w.shape
    w = f64(np.asarray(w, np.float32).astype(ml_dtypes.bfloat16)).reshape(k // 32, 32, n)
    amax = np.abs(w).max(1)
    byte = np.clip(np.where(amax > 0, np.frexp(amax)[1] - 1 + 127 - 7, 1), 1, 254)
    scaled = (w * np.exp2(127.0 - byte)[:, None, :]).reshape(k, n).astype(np.float32)
    words = np.ascontiguousarray(scaled.reshape(k // 512, 128, 4, n).transpose(0, 1, 3, 2)).astype(ml_dtypes.float8_e4m3fn).view(np.uint8)
    return words, np.ascontiguousarray(byte.astype(np.uint8).reshape(k // 512, 16, n))


def unpack_weight(words, scales):
    g, p, n, _ = words.shape
    vals = np.ascontiguousarray(words).view(ml_dtypes.float8_e4m3fn).astype(np.float64) * np.repeat(np.exp2(scales.astype(np.float64) - 127.0), 8, axis=1)[..., None]
    return vals.transpose(0, 1, 3, 2).reshape(g * 512, n)


def relu(v):
    return np.maximum(v, 0.0)


K, T, S, N, G, H = 512, 2048, 512, 512, 2048, 512


def setup_inputs():
    n = np.random.standard_normal
    s = mx_kscale(K)[:, None]
    u = mx_kscale(H)
    packed_xT = pack_weight(n((K, T)) * s)
    packed_dT = pack_weight(n((K, G)) / s)
    return {
        "x_words": packed_xT[0],
        "x_scales": packed_xT[1],
        "d_words": packed_dT[0],
        "d_scales": packed_dT[1],
        "gn": (np.random.uniform(0.5, 1.5, (H, 1)) * u[:, None]).astype(np.float32),
        "w1": (n((H, N)) / np.sqrt(H) / u[:, None]).astype(np.float32),
        "offs": striped(np.random.permutation(T)[:S]),
        "kidx": striped8(np.random.randint(0, G, (8, H))),
        "n1": striped8(np.stack([np.random.permutation(S) for _ in range(8)])),
    }


def reference(x_words, x_scales, d_words, d_scales, gn, w1, offs, kidx, n1):
    d_kidx = unpack_weight(d_words, d_scales)[np.arange(K)[:, None], runs(kidx, K)]
    xq = unpack_weight(x_words, x_scales)[:, unstriped(offs)]
    s = 0.0625 * (d_kidx.T @ xq)
    sq = (s) ** 2
    z = f64(gn) * ((s * relu(s)) / (sq + sq[np.arange(H)[:, None], runs(n1, H)] + 0.25))
    return mxq(f64(w1), 0, "e4m3").T @ mxq(z, 0, "e4m3")

@@ -1,0 +1,227 @@
+from contextlib import ExitStack
+
+import concourse.mybir as mybir
+
+F32 = mybir.dt.float32
+BF16 = mybir.dt.bfloat16
+I32 = mybir.dt.int32
+U32 = mybir.dt.uint32
+U16 = mybir.dt.uint16
+U8 = mybir.dt.uint8
+FP8X4 = mybir.dt.float8_e4m3fn_x4
+ALU = mybir.AluOpType
+ACT = mybir.ActivationFunctionType
+
+P = 128
+PACK = 4
+TABLE = 2048
+KEYS = 512
+QUERIES = 512
+OUT_ROWS = 512
+HALF = QUERIES // 2
+LIST_COLS = 512 // 16
+LAST = PACK - 1
+CHUNKS = ((0, 256), (256, 384), (384, 512))
+
+FLOPS = 2 * 2 * 512 * 512 * 512
+
+
+def tile_picked_scoreshare_none_p_kernel(
+    tc, x_words, x_scales, d_words, d_scales, gn, w1, offs, kidx, n1, out
+):
+    nc = tc.nc
+    with ExitStack() as ctx:
+        keep = ctx.enter_context(tc.tile_pool(name="keep", bufs=1))
+        psum = ctx.enter_context(tc.psum_pool(name="psum", bufs=1))
+
+        def tile(shape, dtype, name, tag=None):
+            return keep.tile(shape, dtype, name=name, tag=tag or name, align_bytes=64)
+
+        kidx_sb = keep.tile([P, LIST_COLS], U16, name="kidx_sb")
+        offs_sb = keep.tile([P, LIST_COLS], U16, name="offs_sb")
+        n1_sb = keep.tile([P, LIST_COLS], U16, name="n1_sb")
+        d_byte_table = tile([P, TABLE], U8, "d_byte_table")
+        x_byte_table = tile([P, TABLE], U8, "x_byte_table")
+        d_word_table = tile([P, TABLE], U32, "d_word_table")
+        x_word_table = tile([P, TABLE], U32, "x_word_table")
+        w_raw = tile([P, PACK, OUT_ROWS], F32, "w_raw")
+        gn_sb = tile([P, PACK], F32, "gn_sb")
+        planes = tile([P, KEYS + QUERIES], U8, "planes")
+
+        nc.vector.memset(d_byte_table[:].bitcast(I32), 0)
+        nc.vector.memset(x_byte_table[:].bitcast(I32), 0)
+        nc.vector.memset(planes[:].bitcast(I32), 0)
+
+        nc.sync.dma_start(kidx_sb[:], kidx)
+        nc.scalar.dma_start(d_byte_table[0:P:8, :].bitcast(I32), d_scales[0].bitcast(I32))
+        nc.sync.dma_start(offs_sb[:], offs)
+        nc.scalar.dma_start(x_byte_table[0:P:8, :].bitcast(I32), x_scales[0].bitcast(I32))
+        nc.sync.dma_start(n1_sb[:], n1)
+        nc.sync.dma_start(gn_sb[:], gn.rearrange("(p t) o -> p (t o)", t=PACK))
+        nc.sync.dma_start(d_word_table[:].bitcast(I32), d_words[0].rearrange("p n t -> p (n t)").bitcast(I32))
+        nc.sync.dma_start(x_word_table[:].bitcast(I32), x_words[0].rearrange("p n t -> p (n t)").bitcast(I32))
+        nc.sync.dma_start(w_raw[:], w1.rearrange("(p j) m -> p j m", j=PACK))
+
+        d_bytes = tile([P, KEYS], U8, "d_bytes")
+        x_bytes = tile([P, QUERIES], U8, "x_bytes")
+        staged = tile([P, KEYS + QUERIES], U8, "staged")
+        nc.vector.tensor_copy(d_bytes[:], d_byte_table[:].indirect(kidx_sb[:]))
+        nc.vector.tensor_copy(
+            staged[:, 0:KEYS].rearrange("p (t m) -> p t m", t=PACK),
+            d_bytes[:].rearrange("p (m t) -> p t m", t=PACK),
+        )
+        nc.vector.tensor_copy(x_bytes[:], x_byte_table[:].indirect(offs_sb[:]))
+        nc.vector.tensor_copy(staged[:, KEYS:].bitcast(I32), x_bytes[:].bitcast(I32))
+        for q in range(4):
+            nc.scalar.dma_start(
+                planes[32 * q : 32 * q + 4, :].bitcast(I32),
+                staged[32 * q : 32 * q + 32 : 8, :].bitcast(I32),
+            )
+
+        d_picked = tile([P, KEYS], U32, "d_picked", tag="x_bytes")
+        d_dealt = tile([P, KEYS], U32, "d_dealt", tag="d_bytes")
+        nc.vector.tensor_copy(d_picked[:], d_word_table[:].indirect(kidx_sb[:]))
+        nc.vector.tensor_copy(
+            d_dealt[:].rearrange("p (t m) -> p m t", t=PACK),
+            d_picked[:].rearrange("p (m t) -> p m t", t=PACK),
+        )
+        x_picked = [tile([P, HALF], U32, "x_picked0", tag="x_bytes"), tile([P, HALF], U32, "x_picked1")]
+        scores = {}
+        sq = [tile([P, QUERIES], F32, "sq%d" % t) for t in range(PACK)]
+        for h in range(2):
+            entries = slice(h * HALF // 16, (h + 1) * HALF // 16)
+            nc.vector.tensor_copy(x_picked[h][:], x_word_table[:].indirect(offs_sb[:, entries]))
+            for t in range(PACK):
+                scores[t, h] = psum.tile([P, HALF], F32, name="bank%d%d" % (t, h))
+                nc.tensor.matmul_mx(
+                    out=scores[t, h][:],
+                    lhsT=d_dealt[:, t * P : (t + 1) * P].bitcast(FP8X4),
+                    lhsT_scale=planes[:, t * P : (t + 1) * P],
+                    rhs=x_picked[h][:].bitcast(FP8X4),
+                    rhs_scale=planes[:, KEYS + h * HALF : KEYS + (h + 1) * HALF],
+                    start=True,
+                    stop=True,
+                )
+
+        w_grouped = tile([P, OUT_ROWS, PACK], BF16, "w_grouped", tag="x_word_table")
+        w_codes = tile([P, OUT_ROWS], U32, "w_codes")
+        w_plane = tile([P, OUT_ROWS], U8, "w_plane")
+
+        def group_weights():
+            nc.vector.tensor_copy(
+                w_grouped[:].rearrange("p (c i) j -> p c j i", i=4),
+                w_raw[:].rearrange("p j (c i) -> p c j i", i=4),
+            )
+
+        def quantize_weights():
+            nc.vector.quantize_mx(w_codes[:].bitcast(FP8X4), w_plane[:], w_grouped[:].rearrange("p m j -> p (m j)"))
+
+        z = tile([P, PACK, QUERIES], F32, "z")
+        other = [tile([P, QUERIES], F32, "other%d" % t) for t in range(PACK)]
+        den = [tile([P, QUERIES], F32, "den%d" % t) for t in range(PACK)]
+        root = [tile([P, QUERIES], F32, "root%d" % t) for t in range(PACK)]
+        u = [tile([P, QUERIES], F32, "u%d" % t) for t in range(PACK)]
+
+        def square(t, h):
+            nc.scalar.activation(sq[t][:, h * HALF : (h + 1) * HALF], scores[t, h][:], ACT.Square, scale=0.0625)
+
+        def fetch(t, a, b):
+            nc.scalar.activation(other[t][:, a:b], sq[t][:].indirect(n1_sb[:, a // 16 : b // 16]), ACT.Copy)
+
+        def add_up(t, a, b):
+            nc.vector.scalar_tensor_tensor(den[t][:, a:b], other[t][:, a:b], 0.25, sq[t][:, a:b], ALU.add, ALU.add)
+
+        def own_term(t, a, b):
+            nc.vector.tensor_scalar_add(other[t][:, a:b], sq[t][:, a:b], 0.25)
+
+        def fetch_and_add(t, a, b):
+            nc.vector.tensor_tensor(den[t][:, a:b], sq[t][:].indirect(n1_sb[:, a // 16 : b // 16]), other[t][:, a:b], ALU.add)
+
+        def inverse_root(t, a, b):
+            nc.scalar.activation(root[t][:, a:b], den[t][:, a:b], ACT.Abs_reciprocal_sqrt, scale=256.0)
+
+        def scale_scores(t, a, b):
+            h = a // HALF
+            nc.vector.scalar_tensor_tensor(
+                u[t][:, a:b], scores[t, h][:, a - h * HALF : b - h * HALF], 0.0, root[t][:, a:b], ALU.max, ALU.mult
+            )
+
+        def weigh(t, a, b):
+            nc.vector.scalar_tensor_tensor(z[:, t, a:b], u[t][:, a:b], gn_sb[:, t : t + 1], u[t][:, a:b], ALU.mult, ALU.mult)
+
+        z_grouped = {}
+
+        def group(a, b, copy):
+            z_grouped[a] = tile([P, b - a, PACK], BF16, "z_grouped%d" % a)
+            copy(
+                z_grouped[a][:].rearrange("p (c i) t -> p c t i", i=4),
+                z[:, :, a:b].rearrange("p t (c i) -> p c t i", i=4),
+            )
+
+        def multiply(a, b, banks, engines):
+            n = b - a
+            z_codes = tile([P, n], U32, "z_codes%d" % a)
+            z_plane = tile([P, n], U8, "z_plane%d" % a)
+            nc.vector.quantize_mx(z_codes[:].bitcast(FP8X4), z_plane[:], z_grouped[a][:].rearrange("p j t -> p (j t)"))
+            blocks = OUT_ROWS // P // len(banks)
+            for part, (bank, engine) in enumerate(zip(banks, engines)):
+                acc = psum.tile([P, blocks, n], F32, name=bank)
+                for i in range(blocks):
+                    rows = slice((part * blocks + i) * P, (part * blocks + i + 1) * P)
+                    nc.tensor.matmul_mx(
+                        out=acc[:, i, :],
+                        lhsT=w_codes[:, rows].bitcast(FP8X4),
+                        lhsT_scale=w_plane[:, rows],
+                        rhs=z_codes[:].bitcast(FP8X4),
+                        rhs_scale=z_plane[:],
+                        start=True,
+                        stop=True,
+                    )
+                result = tile([P, blocks, n], F32, "result%d%d" % (a, part))
+                engine(result[:], acc[:])
+                rows = slice(part * blocks * P, (part + 1) * blocks * P)
+                nc.sync.dma_start(out[rows, a:b].rearrange("(i p) j -> p i j", p=P), result[:])
+
+        halves = ((0, HALF), (HALF, QUERIES))
+        first, second, third = CHUNKS
+        square(0, 0)
+        square(1, 0)
+        square(2, 0)
+        square(0, 1)
+        for half in halves:
+            own_term(0, *half)
+        for half in halves:
+            fetch_and_add(0, *half)
+        for t in range(1, PACK):
+            if t == LAST:
+                square(t, 0)
+            square(t, 1)
+            for part in halves if t < LAST else CHUNKS:
+                fetch(t, *part)
+            inverse_root(t - 1, 0, QUERIES)
+            if t < LAST:
+                add_up(t, 0, QUERIES)
+            else:
+                for part in CHUNKS:
+                    add_up(t, *part)
+            if t == 1:
+                group_weights()
+            for step in (scale_scores, weigh):
+                for half in halves:
+                    step(t - 1, *half)
+            if t == 1:
+                quantize_weights()
+        for part in CHUNKS:
+            inverse_root(LAST, *part)
+        scale_scores(LAST, *first)
+        scale_scores(LAST, *second)
+        weigh(LAST, *first)
+        group(*first, nc.scalar.copy)
+        scale_scores(LAST, *third)
+        weigh(LAST, *second)
+        weigh(LAST, *third)
+        group(*second, nc.vector.tensor_copy)
+        multiply(*first, ("bank00", "bank01"), (nc.scalar.copy, nc.scalar.copy))
+        group(*third, nc.vector.tensor_copy)
+        multiply(*second, ("bank10",), (nc.scalar.copy,))
+        multiply(*third, ("bank11", "bank20"), (nc.scalar.copy, nc.vector.tensor_copy))

@@ -44,23 +44,23 @@ def tile_picked_scoreshare_none_p_kernel(
         x_byte_table = tile([P, TABLE], U8, "x_byte_table")
         d_word_table = tile([P, TABLE], U32, "d_word_table")
         x_word_table = tile([P, TABLE], U32, "x_word_table")
-        w_raw = tile([P, PACK, OUT_ROWS], F32, "w_raw")
         gn_sb = tile([P, PACK], F32, "gn_sb")
         planes = tile([P, KEYS + QUERIES], U8, "planes")
 
-        nc.vector.memset(d_byte_table[:].bitcast(I32), 0)
-        nc.vector.memset(x_byte_table[:].bitcast(I32), 0)
         nc.vector.memset(planes[:].bitcast(I32), 0)
+        warm_in = tile([P, 1], F32, "warm_in")
+        warm_out = tile([P, 1], F32, "warm_out")
+        nc.gpsimd.memset(warm_in[:], 1.0)
+        nc.scalar.activation(warm_out[:], warm_in[:], ACT.Abs_reciprocal_sqrt)
 
         nc.sync.dma_start(kidx_sb[:], kidx)
-        nc.scalar.dma_start(d_byte_table[0:P:8, :].bitcast(I32), d_scales[0].bitcast(I32))
+        nc.sync.dma_start(d_byte_table[:].bitcast(I32), d_scales[0].bitcast(I32).unsqueeze(1).to_broadcast([16, 8, TABLE // 4]))
         nc.sync.dma_start(offs_sb[:], offs)
-        nc.scalar.dma_start(x_byte_table[0:P:8, :].bitcast(I32), x_scales[0].bitcast(I32))
+        nc.sync.dma_start(x_byte_table[:].bitcast(I32), x_scales[0].bitcast(I32).unsqueeze(1).to_broadcast([16, 8, TABLE // 4]))
         nc.sync.dma_start(n1_sb[:], n1)
         nc.sync.dma_start(gn_sb[:], gn.rearrange("(p t) o -> p (t o)", t=PACK))
         nc.sync.dma_start(d_word_table[:].bitcast(I32), d_words[0].rearrange("p n t -> p (n t)").bitcast(I32))
         nc.sync.dma_start(x_word_table[:].bitcast(I32), x_words[0].rearrange("p n t -> p (n t)").bitcast(I32))
-        nc.sync.dma_start(w_raw[:], w1.rearrange("(p j) m -> p j m", j=PACK))
 
         d_bytes = tile([P, KEYS], U8, "d_bytes")
         x_bytes = tile([P, QUERIES], U8, "x_bytes")
@@ -78,30 +78,39 @@ def tile_picked_scoreshare_none_p_kernel(
                 staged[32 * q : 32 * q + 32 : 8, :].bitcast(I32),
             )
 
-        d_picked = tile([P, KEYS], U32, "d_picked", tag="x_bytes")
+        w_raw = tile([P, PACK, OUT_ROWS], F32, "w_raw", tag="x_bytes")
+        nc.scalar.dma_start(w_raw[:], w1.rearrange("(p j) m -> p j m", j=PACK))
+
+        d_picked = tile([P, KEYS], U32, "d_picked", tag="x_byte_table")
         d_dealt = tile([P, KEYS], U32, "d_dealt", tag="d_bytes")
         nc.vector.tensor_copy(d_picked[:], d_word_table[:].indirect(kidx_sb[:]))
         nc.vector.tensor_copy(
             d_dealt[:].rearrange("p (t m) -> p m t", t=PACK),
             d_picked[:].rearrange("p (m t) -> p m t", t=PACK),
         )
-        x_picked = [tile([P, HALF], U32, "x_picked0", tag="x_bytes"), tile([P, HALF], U32, "x_picked1")]
-        scores = {}
+        x_picked = tile([P, QUERIES], U32, "x_picked", tag="x_byte_table")
+        halves = ((0, HALF), (HALF, QUERIES))
+        for a, b in halves:
+            nc.vector.tensor_copy(x_picked[:, a:b], x_word_table[:].indirect(offs_sb[:, a // 16 : b // 16]))
         sq = [tile([P, QUERIES], F32, "sq%d" % t) for t in range(PACK)]
-        for h in range(2):
-            entries = slice(h * HALF // 16, (h + 1) * HALF // 16)
-            nc.vector.tensor_copy(x_picked[h][:], x_word_table[:].indirect(offs_sb[:, entries]))
-            for t in range(PACK):
-                scores[t, h] = psum.tile([P, HALF], F32, name="bank%d%d" % (t, h))
+        spans = [halves, halves, ((0, QUERIES),), ((0, QUERIES),)]
+        scores = {}
+        for t in range(PACK):
+            for a, b in spans[t]:
+                scores[t, a] = psum.tile([P, b - a], F32, name="bank%d_%d" % (t, a))
                 nc.tensor.matmul_mx(
-                    out=scores[t, h][:],
+                    out=scores[t, a][:],
                     lhsT=d_dealt[:, t * P : (t + 1) * P].bitcast(FP8X4),
                     lhsT_scale=planes[:, t * P : (t + 1) * P],
-                    rhs=x_picked[h][:].bitcast(FP8X4),
-                    rhs_scale=planes[:, KEYS + h * HALF : KEYS + (h + 1) * HALF],
+                    rhs=x_picked[:, a:b].bitcast(FP8X4),
+                    rhs_scale=planes[:, KEYS + a : KEYS + b],
                     start=True,
                     stop=True,
                 )
+
+        def score_columns(t, a, b):
+            start = max(lo for lo, hi in spans[t] if lo <= a)
+            return scores[t, start][:, a - start : b - start]
 
         w_grouped = tile([P, OUT_ROWS, PACK], BF16, "w_grouped", tag="x_word_table")
         w_codes = tile([P, OUT_ROWS], U32, "w_codes")
@@ -122,8 +131,8 @@ def tile_picked_scoreshare_none_p_kernel(
         root = [tile([P, QUERIES], F32, "root%d" % t) for t in range(PACK)]
         u = [tile([P, QUERIES], F32, "u%d" % t) for t in range(PACK)]
 
-        def square(t, h):
-            nc.scalar.activation(sq[t][:, h * HALF : (h + 1) * HALF], scores[t, h][:], ACT.Square, scale=0.0625)
+        def square(t, a, b):
+            nc.scalar.activation(sq[t][:, a:b], score_columns(t, a, b), ACT.Square, scale=0.0625)
 
         def fetch(t, a, b):
             nc.scalar.activation(other[t][:, a:b], sq[t][:].indirect(n1_sb[:, a // 16 : b // 16]), ACT.Copy)
@@ -141,9 +150,8 @@ def tile_picked_scoreshare_none_p_kernel(
             nc.scalar.activation(root[t][:, a:b], den[t][:, a:b], ACT.Abs_reciprocal_sqrt, scale=256.0)
 
         def scale_scores(t, a, b):
-            h = a // HALF
             nc.vector.scalar_tensor_tensor(
-                u[t][:, a:b], scores[t, h][:, a - h * HALF : b - h * HALF], 0.0, root[t][:, a:b], ALU.max, ALU.mult
+                u[t][:, a:b], score_columns(t, a, b), 0.0, root[t][:, a:b], ALU.max, ALU.mult
             )
 
         def weigh(t, a, b):
@@ -182,35 +190,33 @@ def tile_picked_scoreshare_none_p_kernel(
                 rows = slice(part * blocks * P, (part + 1) * blocks * P)
                 nc.sync.dma_start(out[rows, a:b].rearrange("(i p) j -> p i j", p=P), result[:])
 
-        halves = ((0, HALF), (HALF, QUERIES))
         first, second, third = CHUNKS
-        square(0, 0)
-        square(1, 0)
-        square(2, 0)
-        square(0, 1)
+        for t in range(2):
+            for half in halves:
+                square(t, *half)
         for half in halves:
             own_term(0, *half)
         for half in halves:
             fetch_and_add(0, *half)
         for t in range(1, PACK):
-            if t == LAST:
-                square(t, 0)
-            square(t, 1)
+            if t > 1:
+                square(t, 0, QUERIES)
             for part in halves if t < LAST else CHUNKS:
                 fetch(t, *part)
             inverse_root(t - 1, 0, QUERIES)
-            if t < LAST:
+            if t == 1:
+                add_up(t, 0, QUERIES)
+                group_weights()
+            for span in spans[t - 1]:
+                scale_scores(t - 1, *span)
+            if t == 1:
+                quantize_weights()
+            elif t < LAST:
                 add_up(t, 0, QUERIES)
             else:
                 for part in CHUNKS:
                     add_up(t, *part)
-            if t == 1:
-                group_weights()
-            for step in (scale_scores, weigh):
-                for half in halves:
-                    step(t - 1, *half)
-            if t == 1:
-                quantize_weights()
+            weigh(t - 1, 0, QUERIES)
         for part in CHUNKS:
             inverse_root(LAST, *part)
         scale_scores(LAST, *first)
@@ -221,7 +227,7 @@ def tile_picked_scoreshare_none_p_kernel(
         weigh(LAST, *second)
         weigh(LAST, *third)
         group(*second, nc.vector.tensor_copy)
-        multiply(*first, ("bank00", "bank01"), (nc.scalar.copy, nc.scalar.copy))
+        multiply(*first, ("out0", "out1"), (nc.scalar.copy, nc.scalar.copy))
         group(*third, nc.vector.tensor_copy)
-        multiply(*second, ("bank10",), (nc.scalar.copy,))
-        multiply(*third, ("bank11", "bank20"), (nc.scalar.copy, nc.vector.tensor_copy))
+        multiply(*second, ("bank0_0",), (nc.scalar.copy,))
+        multiply(*third, ("bank0_256", "bank1_0"), (nc.scalar.copy, nc.vector.tensor_copy))

@@ -57,20 +57,21 @@ def tile_picked_scoreshare_none_p_kernel(
         nc.sync.dma_start(d_byte_table[:].bitcast(I32), d_scales[0].bitcast(I32).unsqueeze(1).to_broadcast([16, 8, TABLE // 4]))
         nc.sync.dma_start(offs_sb[:], offs)
         nc.sync.dma_start(x_byte_table[:].bitcast(I32), x_scales[0].bitcast(I32).unsqueeze(1).to_broadcast([16, 8, TABLE // 4]))
-        nc.sync.dma_start(n1_sb[:], n1)
-        nc.sync.dma_start(gn_sb[:], gn.rearrange("(p t) o -> p (t o)", t=PACK))
         nc.sync.dma_start(d_word_table[:].bitcast(I32), d_words[0].rearrange("p n t -> p (n t)").bitcast(I32))
         nc.sync.dma_start(x_word_table[:].bitcast(I32), x_words[0].rearrange("p n t -> p (n t)").bitcast(I32))
+        nc.sync.dma_start(n1_sb[:], n1)
+        nc.sync.dma_start(gn_sb[:], gn.rearrange("(p t) o -> p (t o)", t=PACK))
+        w_rows = w1.rearrange("(p j) m -> p j m", j=PACK)
 
         d_bytes = tile([P, KEYS], U8, "d_bytes")
         x_bytes = tile([P, QUERIES], U8, "x_bytes")
         staged = tile([P, KEYS + QUERIES], U8, "staged")
         nc.vector.tensor_copy(d_bytes[:], d_byte_table[:].indirect(kidx_sb[:]))
+        nc.vector.tensor_copy(x_bytes[:], x_byte_table[:].indirect(offs_sb[:]))
         nc.vector.tensor_copy(
             staged[:, 0:KEYS].rearrange("p (t m) -> p t m", t=PACK),
             d_bytes[:].rearrange("p (m t) -> p t m", t=PACK),
         )
-        nc.vector.tensor_copy(x_bytes[:], x_byte_table[:].indirect(offs_sb[:]))
         nc.vector.tensor_copy(staged[:, KEYS:].bitcast(I32), x_bytes[:].bitcast(I32))
         for q in range(4):
             nc.scalar.dma_start(
@@ -78,8 +79,8 @@ def tile_picked_scoreshare_none_p_kernel(
                 staged[32 * q : 32 * q + 32 : 8, :].bitcast(I32),
             )
 
-        w_raw = tile([P, PACK, OUT_ROWS], F32, "w_raw", tag="x_bytes")
-        nc.scalar.dma_start(w_raw[:], w1.rearrange("(p j) m -> p j m", j=PACK))
+        w_raw = [tile([P, PACK, HALF], F32, "w_raw0", tag="x_bytes")]
+        nc.scalar.dma_start(w_raw[0][:], w_rows[:, :, 0:HALF])
 
         d_picked = tile([P, KEYS], U32, "d_picked", tag="x_byte_table")
         d_dealt = tile([P, KEYS], U32, "d_dealt", tag="d_bytes")
@@ -88,7 +89,9 @@ def tile_picked_scoreshare_none_p_kernel(
             d_dealt[:].rearrange("p (t m) -> p m t", t=PACK),
             d_picked[:].rearrange("p (m t) -> p m t", t=PACK),
         )
-        x_picked = tile([P, QUERIES], U32, "x_picked", tag="x_byte_table")
+        w_raw.append(tile([P, PACK, HALF], F32, "w_raw1", tag="x_byte_table"))
+        nc.sync.dma_start(w_raw[1][:], w_rows[:, :, HALF:OUT_ROWS])
+        x_picked = tile([P, QUERIES], U32, "x_picked")
         halves = ((0, HALF), (HALF, QUERIES))
         for a, b in halves:
             nc.vector.tensor_copy(x_picked[:, a:b], x_word_table[:].indirect(offs_sb[:, a // 16 : b // 16]))
@@ -112,122 +115,113 @@ def tile_picked_scoreshare_none_p_kernel(
             start = max(lo for lo, hi in spans[t] if lo <= a)
             return scores[t, start][:, a - start : b - start]
 
-        w_grouped = tile([P, OUT_ROWS, PACK], BF16, "w_grouped", tag="x_word_table")
-        w_codes = tile([P, OUT_ROWS], U32, "w_codes")
-        w_plane = tile([P, OUT_ROWS], U8, "w_plane")
+        def interleave(copy, grouped, planar):
+            copy(grouped.rearrange("p (c i) t -> p c t i", i=4), planar.rearrange("p t (c i) -> p c t i", i=4))
 
-        def group_weights():
-            nc.vector.tensor_copy(
-                w_grouped[:].rearrange("p (c i) j -> p c j i", i=4),
-                w_raw[:].rearrange("p j (c i) -> p c j i", i=4),
-            )
-
-        def quantize_weights():
-            nc.vector.quantize_mx(w_codes[:].bitcast(FP8X4), w_plane[:], w_grouped[:].rearrange("p m j -> p (m j)"))
+        def quantize(grouped, name):
+            n = grouped.shape[1]
+            codes = tile([P, n], U32, name + "_codes")
+            plane = tile([P, n], U8, name + "_plane")
+            nc.vector.quantize_mx(codes[:].bitcast(FP8X4), plane[:], grouped[:].rearrange("p c t -> p (c t)"))
+            return codes, plane
 
         z = tile([P, PACK, QUERIES], F32, "z")
-        other = [tile([P, QUERIES], F32, "other%d" % t) for t in range(PACK)]
-        den = [tile([P, QUERIES], F32, "den%d" % t) for t in range(PACK)]
-        root = [tile([P, QUERIES], F32, "root%d" % t) for t in range(PACK)]
-        u = [tile([P, QUERIES], F32, "u%d" % t) for t in range(PACK)]
+        other, den, root, u, z_grouped, w_quantized = {}, {}, {}, {}, {}, []
 
         def square(t, a, b):
             nc.scalar.activation(sq[t][:, a:b], score_columns(t, a, b), ACT.Square, scale=0.0625)
 
+        def looked_up(t, a, b):
+            return sq[t][:].indirect(n1_sb[:, a // 16 : b // 16])
+
         def fetch(t, a, b):
-            nc.scalar.activation(other[t][:, a:b], sq[t][:].indirect(n1_sb[:, a // 16 : b // 16]), ACT.Copy)
+            other[t, a] = tile([P, b - a], F32, "other%d_%d" % (t, a))
+            den[t, a] = tile([P, b - a], F32, "den%d_%d" % (t, a))
+            if a < HALF:
+                nc.vector.tensor_scalar_add(other[t, a][:], sq[t][:, a:b], 0.25)
+                nc.vector.tensor_tensor(den[t, a][:], looked_up(t, a, b), other[t, a][:], ALU.add)
+            else:
+                nc.scalar.activation(other[t, a][:], looked_up(t, a, b), ACT.Copy)
 
         def add_up(t, a, b):
-            nc.vector.scalar_tensor_tensor(den[t][:, a:b], other[t][:, a:b], 0.25, sq[t][:, a:b], ALU.add, ALU.add)
-
-        def own_term(t, a, b):
-            nc.vector.tensor_scalar_add(other[t][:, a:b], sq[t][:, a:b], 0.25)
-
-        def fetch_and_add(t, a, b):
-            nc.vector.tensor_tensor(den[t][:, a:b], sq[t][:].indirect(n1_sb[:, a // 16 : b // 16]), other[t][:, a:b], ALU.add)
+            if a >= HALF:
+                nc.vector.scalar_tensor_tensor(den[t, a][:], other[t, a][:], 0.25, sq[t][:, a:b], ALU.add, ALU.add)
 
         def inverse_root(t, a, b):
-            nc.scalar.activation(root[t][:, a:b], den[t][:, a:b], ACT.Abs_reciprocal_sqrt, scale=256.0)
+            root[t, a] = tile([P, b - a], F32, "root%d_%d" % (t, a))
+            nc.scalar.activation(root[t, a][:], den[t, a][:], ACT.Abs_reciprocal_sqrt, scale=256.0)
 
         def scale_scores(t, a, b):
-            nc.vector.scalar_tensor_tensor(
-                u[t][:, a:b], score_columns(t, a, b), 0.0, root[t][:, a:b], ALU.max, ALU.mult
-            )
+            u[t, a] = tile([P, b - a], F32, "u%d_%d" % (t, a))
+            nc.vector.scalar_tensor_tensor(u[t, a][:], score_columns(t, a, b), 0.0, root[t, a][:], ALU.max, ALU.mult)
 
         def weigh(t, a, b):
-            nc.vector.scalar_tensor_tensor(z[:, t, a:b], u[t][:, a:b], gn_sb[:, t : t + 1], u[t][:, a:b], ALU.mult, ALU.mult)
+            nc.vector.scalar_tensor_tensor(z[:, t, a:b], u[t, a][:], gn_sb[:, t : t + 1], u[t, a][:], ALU.mult, ALU.mult)
 
-        z_grouped = {}
-
-        def group(a, b, copy):
+        def group(a, b):
             z_grouped[a] = tile([P, b - a, PACK], BF16, "z_grouped%d" % a)
-            copy(
-                z_grouped[a][:].rearrange("p (c i) t -> p c t i", i=4),
-                z[:, :, a:b].rearrange("p t (c i) -> p c t i", i=4),
-            )
+            interleave(nc.scalar.copy if a < HALF else nc.vector.tensor_copy, z_grouped[a][:], z[:, :, a:b])
 
-        def multiply(a, b, banks, engines):
-            n = b - a
-            z_codes = tile([P, n], U32, "z_codes%d" % a)
-            z_plane = tile([P, n], U8, "z_plane%d" % a)
-            nc.vector.quantize_mx(z_codes[:].bitcast(FP8X4), z_plane[:], z_grouped[a][:].rearrange("p j t -> p (j t)"))
+        def multiply(a, b):
+            banks, engines = WAYS[a]
+            z_codes, z_plane = quantize(z_grouped[a], "z%d" % a)
             blocks = OUT_ROWS // P // len(banks)
             for part, (bank, engine) in enumerate(zip(banks, engines)):
-                acc = psum.tile([P, blocks, n], F32, name=bank)
+                acc = psum.tile([P, blocks, b - a], F32, name=bank)
                 for i in range(blocks):
-                    rows = slice((part * blocks + i) * P, (part * blocks + i + 1) * P)
+                    w_codes, w_plane = w_quantized[(part * blocks + i) // 2]
+                    cols = slice((part * blocks + i) % 2 * P, ((part * blocks + i) % 2 + 1) * P)
                     nc.tensor.matmul_mx(
                         out=acc[:, i, :],
-                        lhsT=w_codes[:, rows].bitcast(FP8X4),
-                        lhsT_scale=w_plane[:, rows],
+                        lhsT=w_codes[:, cols].bitcast(FP8X4),
+                        lhsT_scale=w_plane[:, cols],
                         rhs=z_codes[:].bitcast(FP8X4),
                         rhs_scale=z_plane[:],
                         start=True,
                         stop=True,
                     )
-                result = tile([P, blocks, n], F32, "result%d%d" % (a, part))
+                result = tile([P, blocks, b - a], F32, "result%d_%d" % (a, part))
                 engine(result[:], acc[:])
                 rows = slice(part * blocks * P, (part + 1) * blocks * P)
                 nc.sync.dma_start(out[rows, a:b].rearrange("(i p) j -> p i j", p=P), result[:])
 
-        first, second, third = CHUNKS
+        WAYS = {
+            0: (("out0", "out1"), (nc.scalar.copy, nc.scalar.copy)),
+            256: (("bank0_0", "bank1_0"), (nc.scalar.copy, nc.scalar.copy)),
+            384: (("out0", "out1", "bank0_256", "bank1_256"), (nc.scalar.copy, nc.vector.tensor_copy) * 2),
+        }
         for t in range(2):
             for half in halves:
                 square(t, *half)
-        for half in halves:
-            own_term(0, *half)
-        for half in halves:
-            fetch_and_add(0, *half)
-        for t in range(1, PACK):
-            if t > 1:
-                square(t, 0, QUERIES)
-            for part in halves if t < LAST else CHUNKS:
-                fetch(t, *part)
-            inverse_root(t - 1, 0, QUERIES)
-            if t == 1:
-                add_up(t, 0, QUERIES)
-                group_weights()
-            for span in spans[t - 1]:
-                scale_scores(t - 1, *span)
-            if t == 1:
-                quantize_weights()
-            elif t < LAST:
-                add_up(t, 0, QUERIES)
-            else:
-                for part in CHUNKS:
-                    add_up(t, *part)
-            weigh(t - 1, 0, QUERIES)
-        for part in CHUNKS:
-            inverse_root(LAST, *part)
-        scale_scores(LAST, *first)
-        scale_scores(LAST, *second)
-        weigh(LAST, *first)
-        group(*first, nc.scalar.copy)
-        scale_scores(LAST, *third)
-        weigh(LAST, *second)
-        weigh(LAST, *third)
-        group(*second, nc.vector.tensor_copy)
-        multiply(*first, ("out0", "out1"), (nc.scalar.copy, nc.scalar.copy))
-        group(*third, nc.vector.tensor_copy)
-        multiply(*second, ("bank0_0",), (nc.scalar.copy,))
-        multiply(*third, ("bank0_256", "bank1_0"), (nc.scalar.copy, nc.vector.tensor_copy))
+        w_grouped = tile([P, HALF, PACK], BF16, "w_grouped0", tag="x_word_table")
+        interleave(nc.vector.tensor_copy, w_grouped[:], w_raw[0][:])
+        w_quantized.append(quantize(w_grouped, "w0"))
+
+        units = [(t, 0, HALF) for t in range(PACK)] + [(t, HALF, QUERIES) for t in range(LAST)]
+        units = units + [(LAST, 256, 384), (LAST, 384, 512)]
+        for step in range(len(units) + 3):
+            now, one_back, two_back, three_back = (
+                units[step - k] if 0 <= step - k < len(units) else None for k in range(4)
+            )
+            if step in (2, 3):
+                square(step, 0, QUERIES)
+            if now:
+                fetch(*now)
+            if one_back:
+                inverse_root(*one_back)
+            if now:
+                add_up(*now)
+            if step == 5:
+                w_grouped = tile([P, HALF, PACK], BF16, "w_grouped1", tag="den1_0")
+                for a in (0, P):
+                    interleave(nc.scalar.copy, w_grouped[:, a : a + P, :], w_raw[1][:, :, a : a + P])
+            if one_back:
+                scale_scores(*one_back)
+            if step == 6:
+                w_quantized.append(quantize(w_grouped, "w1"))
+            if two_back:
+                weigh(*two_back)
+                if two_back[0] == LAST:
+                    group(*two_back[1:])
+            if three_back and three_back[0] == LAST:
+                multiply(*three_back[1:])

@@ -14,14 +14,20 @@ ACT = mybir.ActivationFunctionType
 
 P = 128
 PACK = 4
+LAST = PACK - 1
 TABLE = 2048
+BLOCKS = 16
 KEYS = 512
 QUERIES = 512
 OUT_ROWS = 512
-HALF = QUERIES // 2
-LIST_COLS = 512 // 16
-LAST = PACK - 1
-CHUNKS = ((0, 256), (256, 384), (384, 512))
+HALF = 256
+QUARTER = 128
+GROUP = 16
+SCORE_SCALE = 0.0625
+
+UNITS_FETCHED_BY_VECTOR = 2
+FIRST_TILE_IN_QUARTERS = 2
+SECOND_WEIGHTS_STEP = 3
 
 FLOPS = 2 * 2 * 512 * 512 * 512
 
@@ -37,31 +43,37 @@ def tile_picked_scoreshare_none_p_kernel(
         def tile(shape, dtype, name, tag=None):
             return keep.tile(shape, dtype, name=name, tag=tag or name, align_bytes=64)
 
-        kidx_sb = keep.tile([P, LIST_COLS], U16, name="kidx_sb")
-        offs_sb = keep.tile([P, LIST_COLS], U16, name="offs_sb")
-        n1_sb = keep.tile([P, LIST_COLS], U16, name="n1_sb")
+        kidx_sb = keep.tile([P, KEYS // GROUP], U16, name="kidx_sb")
+        offs_sb = keep.tile([P, QUERIES // GROUP], U16, name="offs_sb")
+        n1_sb = keep.tile([P, QUERIES // GROUP], U16, name="n1_sb")
         d_byte_table = tile([P, TABLE], U8, "d_byte_table")
         x_byte_table = tile([P, TABLE], U8, "x_byte_table")
         d_word_table = tile([P, TABLE], U32, "d_word_table")
         x_word_table = tile([P, TABLE], U32, "x_word_table")
         gn_sb = tile([P, PACK], F32, "gn_sb")
-        planes = tile([P, KEYS + QUERIES], U8, "planes")
 
+        planes = tile([P, KEYS + QUERIES], U8, "planes")
         nc.vector.memset(planes[:].bitcast(I32), 0)
+
         warm_in = tile([P, 1], F32, "warm_in")
         warm_out = tile([P, 1], F32, "warm_out")
         nc.gpsimd.memset(warm_in[:], 1.0)
         nc.scalar.activation(warm_out[:], warm_in[:], ACT.Abs_reciprocal_sqrt)
 
+        def scale_rows(scales):
+            return scales[0].bitcast(I32).unsqueeze(1).to_broadcast([BLOCKS, P // BLOCKS, TABLE // 4])
+
+        def word_rows(words):
+            return words[0].rearrange("p n t -> p (n t)").bitcast(I32)
+
         nc.sync.dma_start(kidx_sb[:], kidx)
-        nc.sync.dma_start(d_byte_table[:].bitcast(I32), d_scales[0].bitcast(I32).unsqueeze(1).to_broadcast([16, 8, TABLE // 4]))
+        nc.sync.dma_start(d_byte_table[:].bitcast(I32), scale_rows(d_scales))
         nc.sync.dma_start(offs_sb[:], offs)
-        nc.sync.dma_start(x_byte_table[:].bitcast(I32), x_scales[0].bitcast(I32).unsqueeze(1).to_broadcast([16, 8, TABLE // 4]))
-        nc.sync.dma_start(d_word_table[:].bitcast(I32), d_words[0].rearrange("p n t -> p (n t)").bitcast(I32))
-        nc.sync.dma_start(x_word_table[:].bitcast(I32), x_words[0].rearrange("p n t -> p (n t)").bitcast(I32))
+        nc.sync.dma_start(x_byte_table[:].bitcast(I32), scale_rows(x_scales))
+        nc.sync.dma_start(d_word_table[:].bitcast(I32), word_rows(d_words))
+        nc.sync.dma_start(x_word_table[:].bitcast(I32), word_rows(x_words))
         nc.sync.dma_start(n1_sb[:], n1)
         nc.sync.dma_start(gn_sb[:], gn.rearrange("(p t) o -> p (t o)", t=PACK))
-        w_rows = w1.rearrange("(p j) m -> p j m", j=PACK)
 
         d_bytes = tile([P, KEYS], U8, "d_bytes")
         x_bytes = tile([P, QUERIES], U8, "x_bytes")
@@ -79,6 +91,7 @@ def tile_picked_scoreshare_none_p_kernel(
                 staged[32 * q : 32 * q + 32 : 8, :].bitcast(I32),
             )
 
+        w_rows = w1.rearrange("(p j) m -> p j m", j=PACK)
         w_raw = [tile([P, PACK, HALF], F32, "w_raw0", tag="x_bytes")]
         nc.scalar.dma_start(w_raw[0][:], w_rows[:, :, 0:HALF])
 
@@ -90,17 +103,17 @@ def tile_picked_scoreshare_none_p_kernel(
             d_picked[:].rearrange("p (m t) -> p m t", t=PACK),
         )
         w_raw.append(tile([P, PACK, HALF], F32, "w_raw1", tag="x_byte_table"))
-        nc.sync.dma_start(w_raw[1][:], w_rows[:, :, HALF:OUT_ROWS])
+        nc.scalar.dma_start(w_raw[1][:], w_rows[:, :, HALF:OUT_ROWS])
         x_picked = tile([P, QUERIES], U32, "x_picked")
         halves = ((0, HALF), (HALF, QUERIES))
         for a, b in halves:
-            nc.vector.tensor_copy(x_picked[:, a:b], x_word_table[:].indirect(offs_sb[:, a // 16 : b // 16]))
-        sq = [tile([P, QUERIES], F32, "sq%d" % t) for t in range(PACK)]
+            nc.vector.tensor_copy(x_picked[:, a:b], x_word_table[:].indirect(offs_sb[:, a // GROUP : b // GROUP]))
+
         spans = [halves, halves, ((0, QUERIES),), ((0, QUERIES),)]
         scores = {}
         for t in range(PACK):
             for a, b in spans[t]:
-                scores[t, a] = psum.tile([P, b - a], F32, name="bank%d_%d" % (t, a))
+                scores[t, a] = psum.tile([P, b - a], F32, name="scores%d_%d" % (t, a))
                 nc.tensor.matmul_mx(
                     out=scores[t, a][:],
                     lhsT=d_dealt[:, t * P : (t + 1) * P].bitcast(FP8X4),
@@ -125,31 +138,35 @@ def tile_picked_scoreshare_none_p_kernel(
             nc.vector.quantize_mx(codes[:].bitcast(FP8X4), plane[:], grouped[:].rearrange("p c t -> p (c t)"))
             return codes, plane
 
+        sq = [tile([P, QUERIES], F32, "sq%d" % t) for t in range(PACK)]
         z = tile([P, PACK, QUERIES], F32, "z")
-        other, den, root, u, z_grouped, w_quantized = {}, {}, {}, {}, {}, []
+        term, den, root, u, z_grouped, w_grouped, w_quantized = {}, {}, {}, {}, {}, {}, {}
 
         def square(t, a, b):
-            nc.scalar.activation(sq[t][:, a:b], score_columns(t, a, b), ACT.Square, scale=0.0625)
+            nc.scalar.activation(sq[t][:, a:b], score_columns(t, a, b), ACT.Square, scale=SCORE_SCALE)
 
         def looked_up(t, a, b):
-            return sq[t][:].indirect(n1_sb[:, a // 16 : b // 16])
+            return sq[t][:].indirect(n1_sb[:, a // GROUP : b // GROUP])
 
-        def fetch(t, a, b):
-            other[t, a] = tile([P, b - a], F32, "other%d_%d" % (t, a))
+        def denominator_tiles(t, a, b):
+            term[t, a] = tile([P, b - a], F32, "term%d_%d" % (t, a))
             den[t, a] = tile([P, b - a], F32, "den%d_%d" % (t, a))
-            if a < HALF:
-                nc.vector.tensor_scalar_add(other[t, a][:], sq[t][:, a:b], 0.25)
-                nc.vector.tensor_tensor(den[t, a][:], looked_up(t, a, b), other[t, a][:], ALU.add)
-            else:
-                nc.scalar.activation(other[t, a][:], looked_up(t, a, b), ACT.Copy)
+
+        def fetch_on_vector(t, a, b):
+            denominator_tiles(t, a, b)
+            nc.vector.tensor_scalar_add(term[t, a][:], sq[t][:, a:b], 0.25)
+            nc.vector.tensor_tensor(den[t, a][:], looked_up(t, a, b), term[t, a][:], ALU.add)
+
+        def fetch_on_scalar(t, a, b):
+            denominator_tiles(t, a, b)
+            nc.scalar.activation(term[t, a][:], looked_up(t, a, b), ACT.Copy)
 
         def add_up(t, a, b):
-            if a >= HALF:
-                nc.vector.scalar_tensor_tensor(den[t, a][:], other[t, a][:], 0.25, sq[t][:, a:b], ALU.add, ALU.add)
+            nc.vector.scalar_tensor_tensor(den[t, a][:], term[t, a][:], 0.25, sq[t][:, a:b], ALU.add, ALU.add)
 
         def inverse_root(t, a, b):
             root[t, a] = tile([P, b - a], F32, "root%d_%d" % (t, a))
-            nc.scalar.activation(root[t, a][:], den[t, a][:], ACT.Abs_reciprocal_sqrt, scale=256.0)
+            nc.scalar.activation(root[t, a][:], den[t, a][:], ACT.Abs_reciprocal_sqrt, scale=SCORE_SCALE**-2)
 
         def scale_scores(t, a, b):
             u[t, a] = tile([P, b - a], F32, "u%d_%d" % (t, a))
@@ -158,70 +175,81 @@ def tile_picked_scoreshare_none_p_kernel(
         def weigh(t, a, b):
             nc.vector.scalar_tensor_tensor(z[:, t, a:b], u[t, a][:], gn_sb[:, t : t + 1], u[t, a][:], ALU.mult, ALU.mult)
 
+        def group_weights(h, tag):
+            w_grouped[h] = tile([P, HALF, PACK], BF16, "w_grouped%d" % h, tag=tag)
+            interleave(nc.vector.tensor_copy, w_grouped[h][:], w_raw[h][:])
+
         def group(a, b):
             z_grouped[a] = tile([P, b - a, PACK], BF16, "z_grouped%d" % a)
             interleave(nc.scalar.copy if a < HALF else nc.vector.tensor_copy, z_grouped[a][:], z[:, :, a:b])
 
+        exits = {
+            0: (("out0", "out1"), (nc.scalar.copy,) * 2),
+            HALF: (("scores0_0", "scores1_0"), (nc.scalar.copy,) * 2),
+            HALF + QUARTER: (
+                ("out0", "out1", "scores0_256", "scores1_256"),
+                (nc.scalar.copy, nc.vector.tensor_copy) * 2,
+            ),
+        }
+
         def multiply(a, b):
-            banks, engines = WAYS[a]
+            banks, copies = exits[a]
             z_codes, z_plane = quantize(z_grouped[a], "z%d" % a)
-            blocks = OUT_ROWS // P // len(banks)
-            for part, (bank, engine) in enumerate(zip(banks, engines)):
-                acc = psum.tile([P, blocks, b - a], F32, name=bank)
-                for i in range(blocks):
-                    w_codes, w_plane = w_quantized[(part * blocks + i) // 2]
-                    cols = slice((part * blocks + i) % 2 * P, ((part * blocks + i) % 2 + 1) * P)
+            per_bank = OUT_ROWS // P // len(banks)
+            for part, (bank, copy) in enumerate(zip(banks, copies)):
+                acc = psum.tile([P, per_bank, b - a], F32, name=bank)
+                first_row = part * per_bank * P
+                for i in range(per_bank):
+                    h, column = divmod(first_row + i * P, HALF)
+                    w_codes, w_plane = w_quantized[h]
                     nc.tensor.matmul_mx(
                         out=acc[:, i, :],
-                        lhsT=w_codes[:, cols].bitcast(FP8X4),
-                        lhsT_scale=w_plane[:, cols],
+                        lhsT=w_codes[:, column : column + P].bitcast(FP8X4),
+                        lhsT_scale=w_plane[:, column : column + P],
                         rhs=z_codes[:].bitcast(FP8X4),
                         rhs_scale=z_plane[:],
                         start=True,
                         stop=True,
                     )
-                result = tile([P, blocks, b - a], F32, "result%d_%d" % (a, part))
-                engine(result[:], acc[:])
-                rows = slice(part * blocks * P, (part + 1) * blocks * P)
-                nc.sync.dma_start(out[rows, a:b].rearrange("(i p) j -> p i j", p=P), result[:])
+                result = tile([P, per_bank, b - a], F32, "result%d_%d" % (a, part))
+                copy(result[:], acc[:])
+                rows = out[first_row : first_row + per_bank * P, a:b]
+                nc.sync.dma_start(rows.rearrange("(i p) j -> p i j", p=P), result[:])
 
-        WAYS = {
-            0: (("out0", "out1"), (nc.scalar.copy, nc.scalar.copy)),
-            256: (("bank0_0", "bank1_0"), (nc.scalar.copy, nc.scalar.copy)),
-            384: (("out0", "out1", "bank0_256", "bank1_256"), (nc.scalar.copy, nc.vector.tensor_copy) * 2),
-        }
-        for t in range(2):
-            for half in halves:
-                square(t, *half)
-        w_grouped = tile([P, HALF, PACK], BF16, "w_grouped0", tag="x_word_table")
-        interleave(nc.vector.tensor_copy, w_grouped[:], w_raw[0][:])
-        w_quantized.append(quantize(w_grouped, "w0"))
+        for t in range(PACK):
+            if spans[t] == halves:
+                for half in halves:
+                    square(t, *half)
+        group_weights(0, "x_word_table")
+        w_quantized[0] = quantize(w_grouped[0], "w0")
 
-        units = [(t, 0, HALF) for t in range(PACK)] + [(t, HALF, QUERIES) for t in range(LAST)]
-        units = units + [(LAST, 256, 384), (LAST, 384, 512)]
-        for step in range(len(units) + 3):
-            now, one_back, two_back, three_back = (
-                units[step - k] if 0 <= step - k < len(units) else None for k in range(4)
-            )
-            if step in (2, 3):
+        quarters = ((HALF, HALF + QUARTER), (HALF + QUARTER, QUERIES))
+        units = (
+            [(t, 0, HALF) for t in range(PACK)]
+            + [(t, HALF, QUERIES) for t in range(FIRST_TILE_IN_QUARTERS)]
+            + [(t, a, b) for a, b in quarters for t in range(FIRST_TILE_IN_QUARTERS, PACK)]
+        )
+
+        for step in range(len(units) + 4):
+            unit = [units[step - back] if 0 <= step - back < len(units) else None for back in range(5)]
+            on_vector = step < UNITS_FETCHED_BY_VECTOR
+            if step < PACK and spans[step] != halves:
                 square(step, 0, QUERIES)
-            if now:
-                fetch(*now)
-            if one_back:
-                inverse_root(*one_back)
-            if now:
-                add_up(*now)
-            if step == 5:
-                w_grouped = tile([P, HALF, PACK], BF16, "w_grouped1", tag="den1_0")
-                for a in (0, P):
-                    interleave(nc.scalar.copy, w_grouped[:, a : a + P, :], w_raw[1][:, :, a : a + P])
-            if one_back:
-                scale_scores(*one_back)
-            if step == 6:
-                w_quantized.append(quantize(w_grouped, "w1"))
-            if two_back:
-                weigh(*two_back)
-                if two_back[0] == LAST:
-                    group(*two_back[1:])
-            if three_back and three_back[0] == LAST:
-                multiply(*three_back[1:])
+            if unit[0]:
+                (fetch_on_vector if on_vector else fetch_on_scalar)(*unit[0])
+            if unit[1]:
+                inverse_root(*unit[1])
+            if unit[0] and not on_vector:
+                add_up(*unit[0])
+            if step == SECOND_WEIGHTS_STEP:
+                group_weights(1, None)
+            if unit[2]:
+                scale_scores(*unit[2])
+            if step == SECOND_WEIGHTS_STEP + 1:
+                w_quantized[1] = quantize(w_grouped[1], "w1")
+            if unit[3]:
+                weigh(*unit[3])
+                if unit[3][0] == LAST:
+                    group(*unit[3][1:])
+            if unit[4] and unit[4][0] == LAST:
+                multiply(*unit[4][1:])

from contextlib import ExitStack

import concourse.mybir as mybir

F32 = mybir.dt.float32
BF16 = mybir.dt.bfloat16
I32 = mybir.dt.int32
U32 = mybir.dt.uint32
U16 = mybir.dt.uint16
U8 = mybir.dt.uint8
FP8X4 = mybir.dt.float8_e4m3fn_x4
ALU = mybir.AluOpType
ACT = mybir.ActivationFunctionType

P = 128
PACK = 4
LAST = PACK - 1
TABLE = 2048
BLOCKS = 16
KEYS = 512
QUERIES = 512
OUT_ROWS = 512
HALF = 256
QUARTER = 128
GROUP = 16
SCORE_SCALE = 0.0625

UNITS_FETCHED_BY_VECTOR = 2
FIRST_TILE_IN_QUARTERS = 2
SECOND_WEIGHTS_STEP = 3

FLOPS = 2 * 2 * 512 * 512 * 512


def tile_picked_scoreshare_none_p_kernel(
    tc, x_words, x_scales, d_words, d_scales, gn, w1, offs, kidx, n1, out
):
    nc = tc.nc
    with ExitStack() as ctx:
        keep = ctx.enter_context(tc.tile_pool(name="keep", bufs=1))
        psum = ctx.enter_context(tc.psum_pool(name="psum", bufs=1))

        def tile(shape, dtype, name, tag=None):
            return keep.tile(shape, dtype, name=name, tag=tag or name, align_bytes=64)

        kidx_sb = keep.tile([P, KEYS // GROUP], U16, name="kidx_sb")
        offs_sb = keep.tile([P, QUERIES // GROUP], U16, name="offs_sb")
        n1_sb = keep.tile([P, QUERIES // GROUP], U16, name="n1_sb")
        d_byte_table = tile([P, TABLE], U8, "d_byte_table")
        x_byte_table = tile([P, TABLE], U8, "x_byte_table")
        d_word_table = tile([P, TABLE], U32, "d_word_table")
        x_word_table = tile([P, TABLE], U32, "x_word_table")
        gn_sb = tile([P, PACK], F32, "gn_sb")

        planes = tile([P, KEYS + QUERIES], U8, "planes")
        nc.vector.memset(planes[:].bitcast(I32), 0)

        warm_in = tile([P, 1], F32, "warm_in")
        warm_out = tile([P, 1], F32, "warm_out")
        nc.gpsimd.memset(warm_in[:], 1.0)
        nc.scalar.activation(warm_out[:], warm_in[:], ACT.Abs_reciprocal_sqrt)

        def scale_rows(scales):
            return scales[0].bitcast(I32).unsqueeze(1).to_broadcast([BLOCKS, P // BLOCKS, TABLE // 4])

        def word_rows(words):
            return words[0].rearrange("p n t -> p (n t)").bitcast(I32)

        nc.sync.dma_start(kidx_sb[:], kidx)
        nc.sync.dma_start(d_byte_table[:].bitcast(I32), scale_rows(d_scales))
        nc.sync.dma_start(offs_sb[:], offs)
        nc.sync.dma_start(x_byte_table[:].bitcast(I32), scale_rows(x_scales))
        nc.sync.dma_start(d_word_table[:].bitcast(I32), word_rows(d_words))
        nc.sync.dma_start(x_word_table[:].bitcast(I32), word_rows(x_words))
        nc.sync.dma_start(n1_sb[:], n1)
        nc.sync.dma_start(gn_sb[:], gn.rearrange("(p t) o -> p (t o)", t=PACK))

        d_bytes = tile([P, KEYS], U8, "d_bytes")
        x_bytes = tile([P, QUERIES], U8, "x_bytes")
        staged = tile([P, KEYS + QUERIES], U8, "staged")
        nc.vector.tensor_copy(d_bytes[:], d_byte_table[:].indirect(kidx_sb[:]))
        nc.vector.tensor_copy(x_bytes[:], x_byte_table[:].indirect(offs_sb[:]))
        nc.vector.tensor_copy(
            staged[:, 0:KEYS].rearrange("p (t m) -> p t m", t=PACK),
            d_bytes[:].rearrange("p (m t) -> p t m", t=PACK),
        )
        nc.vector.tensor_copy(staged[:, KEYS:].bitcast(I32), x_bytes[:].bitcast(I32))
        for q in range(4):
            nc.scalar.dma_start(
                planes[32 * q : 32 * q + 4, :].bitcast(I32),
                staged[32 * q : 32 * q + 32 : 8, :].bitcast(I32),
            )

        w_rows = w1.rearrange("(p j) m -> p j m", j=PACK)
        w_raw = [tile([P, PACK, HALF], F32, "w_raw0", tag="x_bytes")]
        nc.scalar.dma_start(w_raw[0][:], w_rows[:, :, 0:HALF])

        d_picked = tile([P, KEYS], U32, "d_picked", tag="x_byte_table")
        d_dealt = tile([P, KEYS], U32, "d_dealt", tag="d_bytes")
        nc.vector.tensor_copy(d_picked[:], d_word_table[:].indirect(kidx_sb[:]))
        nc.vector.tensor_copy(
            d_dealt[:].rearrange("p (t m) -> p m t", t=PACK),
            d_picked[:].rearrange("p (m t) -> p m t", t=PACK),
        )
        w_raw.append(tile([P, PACK, HALF], F32, "w_raw1", tag="x_byte_table"))
        nc.scalar.dma_start(w_raw[1][:], w_rows[:, :, HALF:OUT_ROWS])
        x_picked = tile([P, QUERIES], U32, "x_picked")
        halves = ((0, HALF), (HALF, QUERIES))
        for a, b in halves:
            nc.vector.tensor_copy(x_picked[:, a:b], x_word_table[:].indirect(offs_sb[:, a // GROUP : b // GROUP]))

        spans = [halves, halves, ((0, QUERIES),), ((0, QUERIES),)]
        scores = {}
        for t in range(PACK):
            for a, b in spans[t]:
                scores[t, a] = psum.tile([P, b - a], F32, name="scores%d_%d" % (t, a))
                nc.tensor.matmul_mx(
                    out=scores[t, a][:],
                    lhsT=d_dealt[:, t * P : (t + 1) * P].bitcast(FP8X4),
                    lhsT_scale=planes[:, t * P : (t + 1) * P],
                    rhs=x_picked[:, a:b].bitcast(FP8X4),
                    rhs_scale=planes[:, KEYS + a : KEYS + b],
                    start=True,
                    stop=True,
                )

        def score_columns(t, a, b):
            start = max(lo for lo, hi in spans[t] if lo <= a)
            return scores[t, start][:, a - start : b - start]

        def interleave(copy, grouped, planar):
            copy(grouped.rearrange("p (c i) t -> p c t i", i=4), planar.rearrange("p t (c i) -> p c t i", i=4))

        def quantize(grouped, name):
            n = grouped.shape[1]
            codes = tile([P, n], U32, name + "_codes")
            plane = tile([P, n], U8, name + "_plane")
            nc.vector.quantize_mx(codes[:].bitcast(FP8X4), plane[:], grouped[:].rearrange("p c t -> p (c t)"))
            return codes, plane

        sq = [tile([P, QUERIES], F32, "sq%d" % t) for t in range(PACK)]
        z = tile([P, PACK, QUERIES], F32, "z")
        term, den, root, u, z_grouped, w_grouped, w_quantized = {}, {}, {}, {}, {}, {}, {}

        def square(t, a, b):
            nc.scalar.activation(sq[t][:, a:b], score_columns(t, a, b), ACT.Square, scale=SCORE_SCALE)

        def looked_up(t, a, b):
            return sq[t][:].indirect(n1_sb[:, a // GROUP : b // GROUP])

        def denominator_tiles(t, a, b):
            term[t, a] = tile([P, b - a], F32, "term%d_%d" % (t, a))
            den[t, a] = tile([P, b - a], F32, "den%d_%d" % (t, a))

        def fetch_on_vector(t, a, b):
            denominator_tiles(t, a, b)
            nc.vector.tensor_scalar_add(term[t, a][:], sq[t][:, a:b], 0.25)
            nc.vector.tensor_tensor(den[t, a][:], looked_up(t, a, b), term[t, a][:], ALU.add)

        def fetch_on_scalar(t, a, b):
            denominator_tiles(t, a, b)
            nc.scalar.activation(term[t, a][:], looked_up(t, a, b), ACT.Copy)

        def add_up(t, a, b):
            nc.vector.scalar_tensor_tensor(den[t, a][:], term[t, a][:], 0.25, sq[t][:, a:b], ALU.add, ALU.add)

        def inverse_root(t, a, b):
            root[t, a] = tile([P, b - a], F32, "root%d_%d" % (t, a))
            nc.scalar.activation(root[t, a][:], den[t, a][:], ACT.Abs_reciprocal_sqrt, scale=SCORE_SCALE**-2)

        def scale_scores(t, a, b):
            u[t, a] = tile([P, b - a], F32, "u%d_%d" % (t, a))
            nc.vector.scalar_tensor_tensor(u[t, a][:], score_columns(t, a, b), 0.0, root[t, a][:], ALU.max, ALU.mult)

        def weigh(t, a, b):
            nc.vector.scalar_tensor_tensor(z[:, t, a:b], u[t, a][:], gn_sb[:, t : t + 1], u[t, a][:], ALU.mult, ALU.mult)

        def group_weights(h, tag):
            w_grouped[h] = tile([P, HALF, PACK], BF16, "w_grouped%d" % h, tag=tag)
            interleave(nc.vector.tensor_copy, w_grouped[h][:], w_raw[h][:])

        def group(a, b):
            z_grouped[a] = tile([P, b - a, PACK], BF16, "z_grouped%d" % a)
            interleave(nc.scalar.copy if a < HALF else nc.vector.tensor_copy, z_grouped[a][:], z[:, :, a:b])

        exits = {
            0: (("out0", "out1"), (nc.scalar.copy,) * 2),
            HALF: (("scores0_0", "scores1_0"), (nc.scalar.copy,) * 2),
            HALF + QUARTER: (
                ("out0", "out1", "scores0_256", "scores1_256"),
                (nc.scalar.copy, nc.vector.tensor_copy) * 2,
            ),
        }

        def multiply(a, b):
            banks, copies = exits[a]
            z_codes, z_plane = quantize(z_grouped[a], "z%d" % a)
            per_bank = OUT_ROWS // P // len(banks)
            for part, (bank, copy) in enumerate(zip(banks, copies)):
                acc = psum.tile([P, per_bank, b - a], F32, name=bank)
                first_row = part * per_bank * P
                for i in range(per_bank):
                    h, column = divmod(first_row + i * P, HALF)
                    w_codes, w_plane = w_quantized[h]
                    nc.tensor.matmul_mx(
                        out=acc[:, i, :],
                        lhsT=w_codes[:, column : column + P].bitcast(FP8X4),
                        lhsT_scale=w_plane[:, column : column + P],
                        rhs=z_codes[:].bitcast(FP8X4),
                        rhs_scale=z_plane[:],
                        start=True,
                        stop=True,
                    )
                result = tile([P, per_bank, b - a], F32, "result%d_%d" % (a, part))
                copy(result[:], acc[:])
                rows = out[first_row : first_row + per_bank * P, a:b]
                nc.sync.dma_start(rows.rearrange("(i p) j -> p i j", p=P), result[:])

        for t in range(PACK):
            if spans[t] == halves:
                for half in halves:
                    square(t, *half)
        group_weights(0, "x_word_table")
        w_quantized[0] = quantize(w_grouped[0], "w0")

        quarters = ((HALF, HALF + QUARTER), (HALF + QUARTER, QUERIES))
        units = (
            [(t, 0, HALF) for t in range(PACK)]
            + [(t, HALF, QUERIES) for t in range(FIRST_TILE_IN_QUARTERS)]
            + [(t, a, b) for a, b in quarters for t in range(FIRST_TILE_IN_QUARTERS, PACK)]
        )

        for step in range(len(units) + 4):
            unit = [units[step - back] if 0 <= step - back < len(units) else None for back in range(5)]
            on_vector = step < UNITS_FETCHED_BY_VECTOR
            if step < PACK and spans[step] != halves:
                square(step, 0, QUERIES)
            if unit[0]:
                (fetch_on_vector if on_vector else fetch_on_scalar)(*unit[0])
            if unit[1]:
                inverse_root(*unit[1])
            if unit[0] and not on_vector:
                add_up(*unit[0])
            if step == SECOND_WEIGHTS_STEP:
                group_weights(1, None)
            if unit[2]:
                scale_scores(*unit[2])
            if step == SECOND_WEIGHTS_STEP + 1:
                w_quantized[1] = quantize(w_grouped[1], "w1")
            if unit[3]:
                weigh(*unit[3])
                if unit[3][0] == LAST:
                    group(*unit[3][1:])
            if unit[4] and unit[4][0] == LAST:
                multiply(*unit[4][1:])
